import numpy as np
import ml_dtypes


def mxq(x, axis, fmt="e4m3"):
    dtype, down = {"e4m3": (ml_dtypes.float8_e4m3fn, 7), "e5m2": (ml_dtypes.float8_e5m2, 14)}[fmt]
    v = np.moveaxis(np.asarray(x, np.float32).astype(ml_dtypes.bfloat16).astype(np.float64), axis, -1)
    blocks = v.reshape(v.shape[:-1] + (-1, 32))
    amax = np.abs(blocks).max(-1, keepdims=True)
    byte = np.maximum(np.where(amax > 0, np.frexp(amax)[1] - 1 + 127, 0) - down, 1)
    scale = np.exp2(byte - 127.0)
    codes = (blocks / scale).astype(np.float32).astype(dtype).astype(np.float64)
    return np.moveaxis((codes * scale).reshape(v.shape), -1, axis)


WIDE = False


def mx_kscale(k):
    if not WIDE:
        return np.ones(k)
    levels = np.array([10, -10, 5, -5, 0])
    if k % 512:
        return np.exp2(np.random.permutation(np.resize(levels, k // 32))).repeat(32)
    a = np.empty((k // 512, 16))
    for p in range(k // 512):
        a[p, :8] = np.random.permutation(np.resize(levels, 8))
        for g in range(8):
            far = levels[np.abs(levels - a[p, g]) >= 10]
            a[p, g + 8] = far[np.random.randint(len(far))]
    return np.exp2(a.ravel()).repeat(32)


def f64(x):
    return np.asarray(x).astype(np.float64)


def striped(idx):
    return np.tile(idx.reshape(-1, 16).T, (8, 1)).astype(np.uint16)


def unstriped(offs):
    return offs[:16].T.reshape(-1).astype(np.int64)


E2M1 = np.array([0.0, 0.5, 1.0, 1.5, 2.0, 3.0, 4.0, 6.0, -0.0, -0.5, -1.0, -1.5, -2.0, -3.0, -4.0, -6.0])


def pack_weight(w, fmt):
    k, n = w.shape
    w = f64(np.asarray(w, np.float32).astype(ml_dtypes.bfloat16)).reshape(k // 32, 32, n)
    amax = np.abs(w).max(1)
    if fmt == "e4m3":
        byte = np.frexp(amax)[1] - 1 + 127 - 7
    else:
        mant, ex = np.frexp(amax / 6.0)
        byte = np.where(mant > 0.5, ex, ex - 1) + 127
    byte = np.clip(np.where(amax > 0, byte, 1), 1, 254)
    scaled = (w * np.exp2(127.0 - byte)[:, None, :]).reshape(k, n).astype(np.float32)
    by_word = np.ascontiguousarray(scaled.reshape(k // 512, 128, 4, n).transpose(0, 1, 3, 2))
    if fmt == "e4m3":
        words = by_word.astype(ml_dtypes.float8_e4m3fn).view(np.uint8)
    else:
        c = by_word.astype(ml_dtypes.float4_e2m1fn).view(np.uint8) & 0xF
        words = (c[..., 0::2] | (c[..., 1::2] << 4)).reshape(k // 512, 128, 2 * n)
    return np.ascontiguousarray(words), np.ascontiguousarray(byte.astype(np.uint8).reshape(k // 512, 16, n))


def unpack_weight(words, scales, fmt):
    g, _, n = scales.shape
    words = np.ascontiguousarray(words).reshape(g, 128, n, -1)
    if fmt == "e4m3":
        vals = words.view(ml_dtypes.float8_e4m3fn).astype(np.float64)
    else:
        nib = np.empty((g, 128, n, 4), np.uint8)
        nib[..., 0::2] = words & 0xF
        nib[..., 1::2] = words >> 4
        vals = E2M1[nib]
    vals = vals * np.repeat(np.exp2(scales.astype(np.float64) - 127.0), 8, axis=1)[..., None]
    return vals.transpose(0, 1, 3, 2).reshape(g * 512, n)


def relu(v):
    return np.maximum(v, 0.0)


K, T, E, C, H, N, HOT = 512, 640, 10, 128, 512, 256, 5


def by_expert(wq, xq):
    return np.concatenate([wq[e].T @ xq[:, e * C:(e + 1) * C] for e in range(E)], axis=1)


def setup_inputs():
    n = np.random.standard_normal
    s = mx_kscale(K)
    u = mx_kscale(H)
    first = np.random.permutation(np.repeat(np.arange(E), T // E))
    second = (first + 1 + np.random.permutation(np.repeat(np.arange(E - 1), -(-T // (E - 1)))[:T])) % E
    while np.bincount(second, minlength=E).max() != T // E:
        load = np.bincount(second, minlength=E); hi, lo = int(load.argmax()), int(load.argmin())
        t = np.flatnonzero((second == hi) & (first != lo))[0]; second[t] = lo
    slot_token = np.empty(E * C, np.int64); pos = np.empty((2, T), np.int64); fill = np.zeros(E, np.int64)
    place = np.stack([np.random.permutation(C) for _ in range(E)])
    for r, deal in enumerate((first, second)):
        for t in np.random.permutation(T):
            e = deal[t]; j = e * C + place[e, fill[e]]; fill[e] += 1; slot_token[j] = t; pos[r, t] = j
    g = np.random.uniform(0.2, 0.8, T)
    x = pack_weight(n((K, T)) * s[:, None], "e4m3")
    w1h = [pack_weight(m, "e4m3") for m in n((HOT, K, H)) / np.sqrt(K) / s[None, :, None]]
    w3h = [pack_weight(m, "e4m3") for m in n((HOT, K, H)) / np.sqrt(K) / s[None, :, None] * u]
    w2h = [pack_weight(m, "e4m3") for m in n((HOT, H, N)) / np.sqrt(H) / u[None, :, None]]
    w1c = [pack_weight(m, "e2m1") for m in n((E - HOT, K, H)) / np.sqrt(K) / s[None, :, None]]
    w3c = [pack_weight(m, "e2m1") for m in n((E - HOT, K, H)) / np.sqrt(K) / s[None, :, None] * u]
    w2c = [pack_weight(m, "e2m1") for m in n((E - HOT, H, N)) / np.sqrt(H) / u[None, :, None]]
    return {
        "x_words": x[0],
        "x_scales": x[1],
        "w1h_words": np.stack([m[0] for m in w1h]),
        "w1h_scales": np.stack([m[1] for m in w1h]),
        "w3h_words": np.stack([m[0] for m in w3h]),
        "w3h_scales": np.stack([m[1] for m in w3h]),
        "w2h_words": np.stack([m[0] for m in w2h]),
        "w2h_scales": np.stack([m[1] for m in w2h]),
        "w1c_words": np.stack([m[0] for m in w1c]),
        "w1c_scales": np.stack([m[1] for m in w1c]),
        "w3c_words": np.stack([m[0] for m in w3c]),
        "w3c_scales": np.stack([m[1] for m in w3c]),
        "w2c_words": np.stack([m[0] for m in w2c]),
        "w2c_scales": np.stack([m[1] for m in w2c]),
        "gate": np.stack([np.tile(g, (128, 1)), np.tile(1.0 - g, (128, 1))]).astype(np.float32),
        "offs": striped(slot_token),
        "pos1": striped(pos[0]),
        "pos2": striped(pos[1]),
    }


def reference(x_words, x_scales, w1h_words, w1h_scales, w3h_words, w3h_scales, w2h_words, w2h_scales, w1c_words, w1c_scales, w3c_words, w3c_scales, w2c_words, w2c_scales, gate, offs, pos1, pos2):
    w1h = np.stack([unpack_weight(w1h_words[e], w1h_scales[e], "e4m3") for e in range(HOT)])
    w3h = np.stack([unpack_weight(w3h_words[e], w3h_scales[e], "e4m3") for e in range(HOT)])
    w2h = np.stack([unpack_weight(w2h_words[e], w2h_scales[e], "e4m3") for e in range(HOT)])
    w1c = np.stack([unpack_weight(w1c_words[e], w1c_scales[e], "e2m1") for e in range(E - HOT)])
    w3c = np.stack([unpack_weight(w3c_words[e], w3c_scales[e], "e2m1") for e in range(E - HOT)])
    w2c = np.stack([unpack_weight(w2c_words[e], w2c_scales[e], "e2m1") for e in range(E - HOT)])
    idx = unstriped(offs)
    xq = unpack_weight(x_words, x_scales, "e4m3")[:, idx]
    w1 = [*w1h, *w1c]
    w3 = [*w3h, *w3c]
    w2 = [*w2h, *w2c]
    h = relu(by_expert(w1, xq)) * by_expert(w3, xq)
    y = by_expert(w2, mxq(h, 0, "e4m3"))
    out = sum(f64(gate[r, :1]) * y[:, unstriped(p)] for r, p in enumerate((pos1, pos2)))
    return out

@@ -1,0 +1,233 @@
+from contextlib import ExitStack
+
+import concourse.mybir as mybir
+from concourse.masks import make_identity
+
+F32 = mybir.dt.float32
+BF16 = mybir.dt.bfloat16
+I32 = mybir.dt.int32
+U32 = mybir.dt.uint32
+U16 = mybir.dt.uint16
+U8 = mybir.dt.uint8
+FP8X4 = mybir.dt.float8_e4m3fn_x4
+FP4X4 = mybir.dt.float4_e2m1fn_x4
+MULT = mybir.AluOpType.mult
+ADD = mybir.AluOpType.add
+RELU = mybir.ActivationFunctionType.Relu
+
+P = 128
+T, E, C, H, N, HOT = 640, 10, 128, 512, 256, 5
+S = E * C
+FLOPS = 2 * S * (512 * H * 2 + H * N)
+
+ORDER = [5, 6, 7, 8, 9, 0, 1, 2, 3, 4]
+GATHERS = [(5, 6, 0, -1), (6, 8, 1, -1), (8, 10, 2, 0), (0, 2, 3, 0), (2, 4, 1, 2), (4, 5, 0, 3)]
+QUANT_GROUPS = [(5, 7), (7, 9), (9, 10), (0, 2), (2, 3), (3, 4), (4, 5)]
+TOKEN_CHUNKS = [[(0, 640)], [(0, 384), (384, 640)]]
+TURN_LAG = 3
+QUANT_LAG = 4
+
+
+def tile_moe_hot_glu_relu_kernel(
+    tc, x_words, x_scales, w1h_words, w1h_scales, w3h_words, w3h_scales, w2h_words, w2h_scales,
+    w1c_words, w1c_scales, w3c_words, w3c_scales, w2c_words, w2c_scales, gate, offs, pos1, pos2, out,
+):
+    nc = tc.nc
+    with ExitStack() as ctx:
+        keep = ctx.enter_context(tc.tile_pool(name="keep", bufs=1))
+        psum = ctx.enter_context(tc.psum_pool(name="psum", bufs=1))
+
+        def plane(name, width):
+            t = keep.tile([P, HOT, width], U8, name=name, align_bytes=64)
+            nc.vector.memset(t[:].bitcast(I32), 0)
+            return t
+
+        def scale_loads(t, row0, src, width):
+            rows = src.rearrange("e s b c -> b (e s) c").bitcast(I32)
+            dst = t[:].bitcast(I32)
+            return [(dst[row0 + r : P : 32, :, 0 : width // 4], rows[r:16:4, :, :]) for r in range(4)]
+
+        words = {}
+
+        def weight_load(key, src, e0, e1):
+            if key[-1] == "h":
+                view = src.rearrange("e s p c d -> p (e s) (c d)")
+                first = 0
+            else:
+                view = src.rearrange("e s p c -> p (e s) c")
+                first = HOT
+            t = keep.tile([P, e1 - e0, view.shape[2]], U8, name="%s_%d" % (key, e0), align_bytes=64)
+            for e in range(e0, e1):
+                words[(key[:2], first + e)] = t[:, e - e0, :]
+            return (t[:].bitcast(I32), view[:, e0:e1, :].bitcast(I32))
+
+        offs_t = keep.tile([P, S // 16], U16, name="offs_t")
+        pos1_t = keep.tile([P, T // 16], U16, name="pos1_t")
+        pos2_t = keep.tile([P, T // 16], U16, name="pos2_t")
+        x_w = keep.tile([P, T], U32, name="x_w", align_bytes=64)
+        x_plane = keep.tile([P, T], U8, name="x_plane", align_bytes=64)
+
+        nc.sync.dma_start(offs_t[:], offs)
+        nc.sync.dma_start(x_w[:].bitcast(I32), x_words.rearrange("s p t d -> p (s t d)").bitcast(I32))
+        xs_rows = x_scales.rearrange("s b t -> (s b) t").bitcast(I32)
+        for q in range(4):
+            nc.scalar.dma_start(
+                x_plane[:].bitcast(I32)[32 * q : 32 * (q + 1), :],
+                xs_rows[4 * q : 4 * (q + 1), :].unsqueeze(0).broadcast_to([8, 4, T // 4]),
+            )
+        ident = keep.tile([P, P], F32, name="ident")
+        zeros = keep.tile([P, P], F32, name="zeros")
+        nc.vector.memset(zeros[:], 0.0)
+        nc.scalar.activation(ident[:], zeros[:], RELU)
+        make_identity(nc, ident[:], nomemset=True)
+
+        s3c = plane("s3c", H)
+        s1c = plane("s1c", H)
+        s_hot = plane("s_hot", H)
+        s2 = plane("s2", N)
+        s3c_loads = scale_loads(s3c, 0, w3c_scales, H)
+        for dst, src in (
+            s3c_loads[2:] + scale_loads(s_hot, 4, w1h_scales, H) + scale_loads(s_hot, 8, w3h_scales, H)
+            + scale_loads(s2, 0, w2c_scales, N)
+        ):
+            nc.gpsimd.dma_start(dst, src)
+
+        gate_t = [keep.tile([P, T], F32, name="gate%d" % r) for r in range(2)]
+        loads = [weight_load("w1c", w1c_words, 0, 3), weight_load("w3c", w3c_words, 0, 3)]
+        loads += scale_loads(s1c, 0, w1c_scales, H) + s3c_loads[:2]
+        loads += [weight_load("w1c", w1c_words, 3, 5), weight_load("w3c", w3c_words, 3, 5)]
+        for e in range(HOT):
+            loads += [weight_load("w1h", w1h_words, e, e + 1), weight_load("w3h", w3h_words, e, e + 1)]
+        loads += [weight_load("w2c", w2c_words, 0, 5)] + scale_loads(s2, 4, w2h_scales, N)
+        loads += [weight_load("w2h", w2h_words, 0, 3), weight_load("w2h", w2h_words, 3, 5)]
+        loads += [(pos1_t[:], pos1), (gate_t[0][:], gate[0]), (pos2_t[:], pos2), (gate_t[1][:], gate[1])]
+        for dst, src in loads:
+            nc.sync.dma_start(dst, src)
+
+        bank_a = [psum.tile([P, H], F32, name="bank_a%d" % j) for j in range(2)]
+        bank_b = [psum.tile([P, H], F32, name="bank_b%d" % j) for j in range(3)]
+        bank_t = [psum.tile([P, H], F32, name="bank_t%d" % j) for j in range(2)]
+        bank_y = psum.tile([P, H], F32, name="bank_y")
+
+        x_codes = {}
+        x_bytes = {}
+
+        gathered = {}
+
+        def gather(e0, e1, buffer):
+            n = (e1 - e0) * C
+            cols = offs_t[:, e0 * C // 16 : e1 * C // 16]
+            if buffer not in gathered:
+                gathered[buffer] = (
+                    keep.tile([P, n], U8, name="gb%d" % buffer, align_bytes=64),
+                    keep.tile([P, n], U32, name="gw%d" % buffer, align_bytes=64),
+                )
+            gb, gw = gathered[buffer]
+            nc.vector.tensor_copy(gb[:], x_plane[:].indirect(cols))
+            nc.vector.tensor_copy(gw[:], x_w[:].indirect(cols))
+            for e in range(e0, e1):
+                x_codes[e] = gw[:, (e - e0) * C : (e - e0 + 1) * C]
+                x_bytes[e] = gb[:, (e - e0) * C : (e - e0 + 1) * C]
+
+        def fmt(e):
+            return FP8X4 if e < HOT else FP4X4
+
+        h_tiles = {}
+        grouped = {}
+        h_codes = {}
+        h_bytes = {}
+        for e0, e1 in QUANT_GROUPS:
+            grouped[e0] = keep.tile([P, (e1 - e0) * H], BF16, name="grouped%d" % e0, align_bytes=64)
+
+        def first_layer(step):
+            e = ORDER[step]
+            a = bank_a[step % 2]
+            b = bank_b[step % 3]
+            s1 = s_hot[4:P, e, :] if e < HOT else s1c[:, e - HOT, :]
+            s3 = s_hot[8:P, e, :] if e < HOT else s3c[:, e - HOT, :]
+            for acc, key, sc in ((a, "w1", s1), (b, "w3", s3)):
+                nc.tensor.matmul_mx(
+                    acc[:], lhsT=x_codes[e].bitcast(FP8X4), lhsT_scale=x_bytes[e],
+                    rhs=words[(key, e)].bitcast(fmt(e)), rhs_scale=sc, start=True, stop=True,
+                )
+            r = keep.tile([P, H], F32, name="r%d" % e)
+            nc.scalar.activation(
+                r[:].rearrange("s (u p d) -> s u p d", u=2, d=2),
+                a[:].rearrange("s (p u d) -> s u p d", u=2, d=2), RELU,
+            )
+            h = keep.tile([P, H], BF16, name="h%d" % e, align_bytes=64)
+            nc.vector.tensor_tensor(
+                h[:].rearrange("s (u p d) -> s u p d", u=2, d=2),
+                b[:].rearrange("s (p u d) -> s u p d", u=2, d=2),
+                r[:].rearrange("s (u p d) -> s u p d", u=2, d=2), MULT,
+            )
+            h_tiles[e] = h
+
+        def turn(step):
+            e = ORDER[step]
+            e0 = [g for g in QUANT_GROUPS if g[0] <= e < g[1]][0][0]
+            pairs = h_tiles[e][:].bitcast(F32)
+            ht = bank_t[step % 2]
+            for u in range(2):
+                nc.tensor.transpose(ht[:, u * C : (u + 1) * C], pairs[:, u * P : (u + 1) * P], ident[:])
+            nc.scalar.copy(
+                grouped[e0][:, (e - e0) * H : (e - e0 + 1) * H].bitcast(F32).rearrange("p (s u) -> p s u", u=2),
+                ht[:, 0 : 2 * C].rearrange("p (u s) -> p s u", u=2),
+            )
+
+        def quantise(e0, e1):
+            codes = keep.tile([P, (e1 - e0) * C], U32, name="codes%d" % e0, align_bytes=64)
+            scales = keep.tile([P, (e1 - e0) * C], U8, name="scales%d" % e0, align_bytes=64)
+            nc.vector.quantize_mx(codes[:].bitcast(FP8X4), scales[:], grouped[e0][:])
+            for e in range(e0, e1):
+                h_codes[e] = codes[:, (e - e0) * C : (e - e0 + 1) * C]
+                h_bytes[e] = scales[:, (e - e0) * C : (e - e0 + 1) * C]
+
+        y = [keep.tile([P, S], F32, name="y%d" % half) for half in range(2)]
+
+        def second_layer(half, e0, e1, bank, copy):
+            for e in range(e0, e1):
+                w = words[("w2", e)]
+                size = w.shape[1] // 2
+                cols = slice(half * P, (half + 1) * P)
+                sc = s2[4:P, e, cols] if e < HOT else s2[:, e - HOT, cols]
+                nc.tensor.matmul_mx(
+                    bank[:, (e - e0) * C : (e - e0 + 1) * C],
+                    lhsT=w[:, half * size : (half + 1) * size].bitcast(fmt(e)), lhsT_scale=sc,
+                    rhs=h_codes[e].bitcast(FP8X4), rhs_scale=h_bytes[e], start=True, stop=True,
+                )
+            copy(y[half][:, e0 * C : e1 * C], bank[:, 0 : (e1 - e0) * C])
+
+        for step in range(-1, E + QUANT_LAG):
+            if 0 <= step < E:
+                first_layer(step)
+            for e0, e1, buffer, behind in GATHERS:
+                if behind == step:
+                    gather(e0, e1, buffer)
+            if TURN_LAG <= step < E + TURN_LAG:
+                turn(step - TURN_LAG)
+            if step >= QUANT_LAG:
+                e = ORDER[step - QUANT_LAG]
+                for e0, e1 in QUANT_GROUPS:
+                    if e == e1 - 1:
+                        quantise(e0, e1)
+        second_layer(0, 5, 9, bank_y, nc.scalar.copy)
+        second_layer(0, 9, 10, bank_b[1], nc.vector.tensor_copy)
+        second_layer(0, 0, 4, bank_a[0], nc.scalar.copy)
+        second_layer(0, 4, 5, bank_a[1], nc.scalar.copy)
+        second_layer(1, 8, 10, bank_a[1], nc.scalar.copy)
+        second_layer(1, 0, 4, bank_a[0], nc.scalar.copy)
+        second_layer(1, 4, 8, bank_a[1], nc.scalar.copy)
+
+        for half in range(2):
+            for t0, t1 in TOKEN_CHUNKS[half]:
+                parts = []
+                for r, pos_t in enumerate((pos1_t, pos2_t)):
+                    part = keep.tile([P, t1 - t0], F32, name="part%d_%d_%d" % (half, t0, r))
+                    nc.vector.tensor_tensor(
+                        part[:], y[half][:].indirect(pos_t[:, t0 // 16 : t1 // 16]), gate_t[r][:, t0:t1], MULT
+                    )
+                    parts.append(part)
+                res = keep.tile([P, t1 - t0], F32, name="res%d_%d" % (half, t0))
+                nc.vector.tensor_tensor(res[:], parts[0][:], parts[1][:], ADD)
+                nc.sync.dma_start(out[half * P : (half + 1) * P, t0:t1], res[:])

@@ -21,8 +21,10 @@ S = E * C
 FLOPS = 2 * S * (512 * H * 2 + H * N)
 
 ORDER = [5, 6, 7, 8, 9, 0, 1, 2, 3, 4]
-GATHERS = [(5, 6, 0, -1), (6, 8, 1, -1), (8, 10, 2, 0), (0, 2, 3, 0), (2, 4, 1, 2), (4, 5, 0, 3)]
-QUANT_GROUPS = [(5, 7), (7, 9), (9, 10), (0, 2), (2, 3), (3, 4), (4, 5)]
+GATHERS = [(5, 7, 0, -1), (7, 10, 1, -1), (0, 2, 2, 0), (2, 4, 0, 1), (4, 5, 3, 3)]
+B_BANK = [0, 2, 1, 3, 0, 4, 1, 2, 0, 3]
+TURN_GROUPS = [(0, 2), (2, 4), (4, 6), (6, 8), (8, 9), (9, 10)]
+QUANT_GROUPS = [(0, 4), (4, 8), (8, 9), (9, 10)]
 TOKEN_CHUNKS = [[(0, 640)], [(0, 384), (384, 640)]]
 TURN_LAG = 3
 QUANT_LAG = 4
@@ -37,9 +39,9 @@ def tile_moe_hot_glu_relu_kernel(
         keep = ctx.enter_context(tc.tile_pool(name="keep", bufs=1))
         psum = ctx.enter_context(tc.psum_pool(name="psum", bufs=1))
 
-        def plane(name, width):
+        def plane(name, width, engine):
             t = keep.tile([P, HOT, width], U8, name=name, align_bytes=64)
-            nc.vector.memset(t[:].bitcast(I32), 0)
+            engine.memset(t[:].bitcast(I32), 0)
             return t
 
         def scale_loads(t, row0, src, width):
@@ -75,29 +77,27 @@ def tile_moe_hot_glu_relu_kernel(
                 x_plane[:].bitcast(I32)[32 * q : 32 * (q + 1), :],
                 xs_rows[4 * q : 4 * (q + 1), :].unsqueeze(0).broadcast_to([8, 4, T // 4]),
             )
+        s_hot = plane("s_hot", H, nc.gpsimd)
         ident = keep.tile([P, P], F32, name="ident")
         zeros = keep.tile([P, P], F32, name="zeros")
         nc.vector.memset(zeros[:], 0.0)
         nc.scalar.activation(ident[:], zeros[:], RELU)
         make_identity(nc, ident[:], nomemset=True)
 
-        s3c = plane("s3c", H)
-        s1c = plane("s1c", H)
-        s_hot = plane("s_hot", H)
-        s2 = plane("s2", N)
-        s3c_loads = scale_loads(s3c, 0, w3c_scales, H)
-        for dst, src in (
-            s3c_loads[2:] + scale_loads(s_hot, 4, w1h_scales, H) + scale_loads(s_hot, 8, w3h_scales, H)
-            + scale_loads(s2, 0, w2c_scales, N)
-        ):
+        s1c = plane("s1c", H, nc.vector)
+        s3c = plane("s3c", H, nc.vector)
+        s2 = plane("s2", N, nc.vector)
+        for dst, src in scale_loads(s_hot, 4, w1h_scales, H):
+            nc.scalar.dma_start(dst, src)
+        for dst, src in scale_loads(s_hot, 8, w3h_scales, H) + scale_loads(s2, 0, w2c_scales, N):
             nc.gpsimd.dma_start(dst, src)
 
         gate_t = [keep.tile([P, T], F32, name="gate%d" % r) for r in range(2)]
-        loads = [weight_load("w1c", w1c_words, 0, 3), weight_load("w3c", w3c_words, 0, 3)]
-        loads += scale_loads(s1c, 0, w1c_scales, H) + s3c_loads[:2]
-        loads += [weight_load("w1c", w1c_words, 3, 5), weight_load("w3c", w3c_words, 3, 5)]
-        for e in range(HOT):
-            loads += [weight_load("w1h", w1h_words, e, e + 1), weight_load("w3h", w3h_words, e, e + 1)]
+        loads = [weight_load("w1c", w1c_words, 0, 2), weight_load("w3c", w3c_words, 0, 2)]
+        loads += scale_loads(s1c, 0, w1c_scales, H) + scale_loads(s3c, 0, w3c_scales, H)
+        loads += [weight_load("w1c", w1c_words, 2, 5), weight_load("w3c", w3c_words, 2, 5)]
+        for e0, e1 in ((0, 2), (2, 4), (4, 5)):
+            loads += [weight_load("w1h", w1h_words, e0, e1), weight_load("w3h", w3h_words, e0, e1)]
         loads += [weight_load("w2c", w2c_words, 0, 5)] + scale_loads(s2, 4, w2h_scales, N)
         loads += [weight_load("w2h", w2h_words, 0, 3), weight_load("w2h", w2h_words, 3, 5)]
         loads += [(pos1_t[:], pos1), (gate_t[0][:], gate[0]), (pos2_t[:], pos2), (gate_t[1][:], gate[1])]
@@ -105,13 +105,11 @@ def tile_moe_hot_glu_relu_kernel(
             nc.sync.dma_start(dst, src)
 
         bank_a = [psum.tile([P, H], F32, name="bank_a%d" % j) for j in range(2)]
-        bank_b = [psum.tile([P, H], F32, name="bank_b%d" % j) for j in range(3)]
-        bank_t = [psum.tile([P, H], F32, name="bank_t%d" % j) for j in range(2)]
+        bank_b = [psum.tile([P, H], F32, name="bank_b%d" % j) for j in range(5)]
         bank_y = psum.tile([P, H], F32, name="bank_y")
 
         x_codes = {}
         x_bytes = {}
-
         gathered = {}
 
         def gather(e0, e1, buffer):
@@ -136,16 +134,16 @@ def tile_moe_hot_glu_relu_kernel(
         grouped = {}
         h_codes = {}
         h_bytes = {}
-        for e0, e1 in QUANT_GROUPS:
-            grouped[e0] = keep.tile([P, (e1 - e0) * H], BF16, name="grouped%d" % e0, align_bytes=64)
+        for s0, s1 in QUANT_GROUPS:
+            grouped[s0] = keep.tile([P, (s1 - s0) * H], BF16, name="grouped%d" % s0, align_bytes=64)
 
         def first_layer(step):
             e = ORDER[step]
             a = bank_a[step % 2]
-            b = bank_b[step % 3]
-            s1 = s_hot[4:P, e, :] if e < HOT else s1c[:, e - HOT, :]
-            s3 = s_hot[8:P, e, :] if e < HOT else s3c[:, e - HOT, :]
-            for acc, key, sc in ((a, "w1", s1), (b, "w3", s3)):
+            b = bank_b[B_BANK[step]]
+            sc1 = s_hot[4:P, e, :] if e < HOT else s1c[:, e - HOT, :]
+            sc3 = s_hot[8:P, e, :] if e < HOT else s3c[:, e - HOT, :]
+            for acc, key, sc in ((a, "w1", sc1), (b, "w3", sc3)):
                 nc.tensor.matmul_mx(
                     acc[:], lhsT=x_codes[e].bitcast(FP8X4), lhsT_scale=x_bytes[e],
                     rhs=words[(key, e)].bitcast(fmt(e)), rhs_scale=sc, start=True, stop=True,
@@ -161,27 +159,28 @@ def tile_moe_hot_glu_relu_kernel(
                 b[:].rearrange("s (p u d) -> s u p d", u=2, d=2),
                 r[:].rearrange("s (u p d) -> s u p d", u=2, d=2), MULT,
             )
-            h_tiles[e] = h
+            h_tiles[step] = h
 
-        def turn(step):
-            e = ORDER[step]
-            e0 = [g for g in QUANT_GROUPS if g[0] <= e < g[1]][0][0]
-            pairs = h_tiles[e][:].bitcast(F32)
-            ht = bank_t[step % 2]
-            for u in range(2):
-                nc.tensor.transpose(ht[:, u * C : (u + 1) * C], pairs[:, u * P : (u + 1) * P], ident[:])
+        def turn(s0, s1):
+            q0 = [g for g in QUANT_GROUPS if g[0] <= s0 < g[1]][0][0]
+            bank = bank_b[B_BANK[s1 - 1]]
+            for step in range(s0, s1):
+                pairs = h_tiles[step][:].bitcast(F32)
+                for u in range(2):
+                    col = (2 * (step - s0) + u) * C
+                    nc.tensor.transpose(bank[:, col : col + C], pairs[:, u * P : (u + 1) * P], ident[:])
             nc.scalar.copy(
-                grouped[e0][:, (e - e0) * H : (e - e0 + 1) * H].bitcast(F32).rearrange("p (s u) -> p s u", u=2),
-                ht[:, 0 : 2 * C].rearrange("p (u s) -> p s u", u=2),
+                grouped[q0][:, (s0 - q0) * H : (s1 - q0) * H].bitcast(F32).rearrange("p (e s u) -> p e s u", s=C, u=2),
+                bank[:, 0 : (s1 - s0) * 2 * C].rearrange("p (e u s) -> p e s u", s=C, u=2),
             )
 
-        def quantise(e0, e1):
-            codes = keep.tile([P, (e1 - e0) * C], U32, name="codes%d" % e0, align_bytes=64)
-            scales = keep.tile([P, (e1 - e0) * C], U8, name="scales%d" % e0, align_bytes=64)
-            nc.vector.quantize_mx(codes[:].bitcast(FP8X4), scales[:], grouped[e0][:])
-            for e in range(e0, e1):
-                h_codes[e] = codes[:, (e - e0) * C : (e - e0 + 1) * C]
-                h_bytes[e] = scales[:, (e - e0) * C : (e - e0 + 1) * C]
+        def quantise(s0, s1):
+            codes = keep.tile([P, (s1 - s0) * C], U32, name="codes%d" % s0, align_bytes=64)
+            scales = keep.tile([P, (s1 - s0) * C], U8, name="scales%d" % s0, align_bytes=64)
+            nc.vector.quantize_mx(codes[:].bitcast(FP8X4), scales[:], grouped[s0][:])
+            for step in range(s0, s1):
+                h_codes[ORDER[step]] = codes[:, (step - s0) * C : (step - s0 + 1) * C]
+                h_bytes[ORDER[step]] = scales[:, (step - s0) * C : (step - s0 + 1) * C]
 
         y = [keep.tile([P, S], F32, name="y%d" % half) for half in range(2)]
 
@@ -204,16 +203,15 @@ def tile_moe_hot_glu_relu_kernel(
             for e0, e1, buffer, behind in GATHERS:
                 if behind == step:
                     gather(e0, e1, buffer)
-            if TURN_LAG <= step < E + TURN_LAG:
-                turn(step - TURN_LAG)
-            if step >= QUANT_LAG:
-                e = ORDER[step - QUANT_LAG]
-                for e0, e1 in QUANT_GROUPS:
-                    if e == e1 - 1:
-                        quantise(e0, e1)
+            for s0, s1 in TURN_GROUPS:
+                if s1 - 1 + TURN_LAG == step:
+                    turn(s0, s1)
+            for s0, s1 in QUANT_GROUPS:
+                if s1 - 1 + QUANT_LAG == step:
+                    quantise(s0, s1)
         second_layer(0, 5, 9, bank_y, nc.scalar.copy)
-        second_layer(0, 9, 10, bank_b[1], nc.vector.tensor_copy)
-        second_layer(0, 0, 4, bank_a[0], nc.scalar.copy)
+        second_layer(0, 9, 10, bank_b[1], nc.scalar.copy)
+        second_layer(0, 0, 4, bank_a[0], nc.vector.tensor_copy)
         second_layer(0, 4, 5, bank_a[1], nc.scalar.copy)
         second_layer(1, 8, 10, bank_a[1], nc.scalar.copy)
         second_layer(1, 0, 4, bank_a[0], nc.scalar.copy)

@@ -21,11 +21,10 @@ S = E * C
 FLOPS = 2 * S * (512 * H * 2 + H * N)
 
 ORDER = [5, 6, 7, 8, 9, 0, 1, 2, 3, 4]
-GATHERS = [(5, 7, 0, -1), (7, 10, 1, -1), (0, 2, 2, 0), (2, 4, 0, 1), (4, 5, 3, 3)]
+GATHERS = [(5, 7, 0, -1), (7, 10, 1, -1), (0, 3, 2, 0), (3, 5, 0, 1)]
 B_BANK = [0, 2, 1, 3, 0, 4, 1, 2, 0, 3]
 TURN_GROUPS = [(0, 2), (2, 4), (4, 6), (6, 8), (8, 9), (9, 10)]
 QUANT_GROUPS = [(0, 4), (4, 8), (8, 9), (9, 10)]
-TOKEN_CHUNKS = [[(0, 640)], [(0, 384), (384, 640)]]
 TURN_LAG = 3
 QUANT_LAG = 4
 
@@ -69,38 +68,40 @@ def tile_moe_hot_glu_relu_kernel(
         x_w = keep.tile([P, T], U32, name="x_w", align_bytes=64)
         x_plane = keep.tile([P, T], U8, name="x_plane", align_bytes=64)
 
-        nc.sync.dma_start(offs_t[:], offs)
-        nc.sync.dma_start(x_w[:].bitcast(I32), x_words.rearrange("s p t d -> p (s t d)").bitcast(I32))
         xs_rows = x_scales.rearrange("s b t -> (s b) t").bitcast(I32)
+        nc.sync.dma_start(offs_t[:], offs)
         for q in range(4):
-            nc.scalar.dma_start(
+            queue = nc.sync if q == 0 else nc.scalar
+            queue.dma_start(
                 x_plane[:].bitcast(I32)[32 * q : 32 * (q + 1), :],
                 xs_rows[4 * q : 4 * (q + 1), :].unsqueeze(0).broadcast_to([8, 4, T // 4]),
             )
-        s_hot = plane("s_hot", H, nc.gpsimd)
+        nc.sync.dma_start(x_w[:].bitcast(I32), x_words.rearrange("s p t d -> p (s t d)").bitcast(I32))
         ident = keep.tile([P, P], F32, name="ident")
-        zeros = keep.tile([P, P], F32, name="zeros")
-        nc.vector.memset(zeros[:], 0.0)
-        nc.scalar.activation(ident[:], zeros[:], RELU)
-        make_identity(nc, ident[:], nomemset=True)
+        make_identity(nc, ident[:])
+        warm = keep.tile([P, 16], F32, name="warm")
+        nc.vector.memset(warm[:, 0:8], 0.0)
+        nc.scalar.activation(warm[:, 8:16], warm[:, 0:8], RELU)
 
+        s_hot = plane("s_hot", H, nc.vector)
         s1c = plane("s1c", H, nc.vector)
         s3c = plane("s3c", H, nc.vector)
-        s2 = plane("s2", N, nc.vector)
+        s2 = plane("s2", N, nc.gpsimd)
+        s2c_loads = scale_loads(s2, 0, w2c_scales, N)
         for dst, src in scale_loads(s_hot, 4, w1h_scales, H):
             nc.scalar.dma_start(dst, src)
-        for dst, src in scale_loads(s_hot, 8, w3h_scales, H) + scale_loads(s2, 0, w2c_scales, N):
+        for dst, src in scale_loads(s_hot, 8, w3h_scales, H) + s2c_loads[:2]:
             nc.gpsimd.dma_start(dst, src)
 
-        gate_t = [keep.tile([P, T], F32, name="gate%d" % r) for r in range(2)]
+        gate_t = keep.tile([P, 2, T], F32, name="gate_t")
         loads = [weight_load("w1c", w1c_words, 0, 2), weight_load("w3c", w3c_words, 0, 2)]
         loads += scale_loads(s1c, 0, w1c_scales, H) + scale_loads(s3c, 0, w3c_scales, H)
         loads += [weight_load("w1c", w1c_words, 2, 5), weight_load("w3c", w3c_words, 2, 5)]
-        for e0, e1 in ((0, 2), (2, 4), (4, 5)):
-            loads += [weight_load("w1h", w1h_words, e0, e1), weight_load("w3h", w3h_words, e0, e1)]
-        loads += [weight_load("w2c", w2c_words, 0, 5)] + scale_loads(s2, 4, w2h_scales, N)
+        for e in range(HOT):
+            loads += [weight_load("w1h", w1h_words, e, e + 1), weight_load("w3h", w3h_words, e, e + 1)]
+        loads += [weight_load("w2c", w2c_words, 0, 5)] + s2c_loads[2:] + scale_loads(s2, 4, w2h_scales, N)
         loads += [weight_load("w2h", w2h_words, 0, 3), weight_load("w2h", w2h_words, 3, 5)]
-        loads += [(pos1_t[:], pos1), (gate_t[0][:], gate[0]), (pos2_t[:], pos2), (gate_t[1][:], gate[1])]
+        loads += [(pos1_t[:], pos1), (pos2_t[:], pos2), (gate_t[:], gate.rearrange("r p t -> p r t"))]
         for dst, src in loads:
             nc.sync.dma_start(dst, src)
 
@@ -217,15 +218,36 @@ def tile_moe_hot_glu_relu_kernel(
         second_layer(1, 0, 4, bank_a[0], nc.scalar.copy)
         second_layer(1, 4, 8, bank_a[1], nc.scalar.copy)
 
-        for half in range(2):
-            for t0, t1 in TOKEN_CHUNKS[half]:
-                parts = []
-                for r, pos_t in enumerate((pos1_t, pos2_t)):
-                    part = keep.tile([P, t1 - t0], F32, name="part%d_%d_%d" % (half, t0, r))
-                    nc.vector.tensor_tensor(
-                        part[:], y[half][:].indirect(pos_t[:, t0 // 16 : t1 // 16]), gate_t[r][:, t0:t1], MULT
+        def weighted(half, t0, t1):
+            parts = []
+            for r, pos_t in enumerate((pos1_t, pos2_t)):
+                part = keep.tile([P, t1 - t0], F32, name="part%d_%d_%d" % (half, t0, r))
+                nc.vector.tensor_tensor(
+                    part[:], y[half][:].indirect(pos_t[:, t0 // 16 : t1 // 16]), gate_t[:, r, t0:t1], MULT
+                )
+                parts.append(part)
+            return parts
+
+        def add_on_tensor(half, t0, parts, c0, c1, bank_sum, bank_back):
+            width = c1 - c0
+            for c in range(0, width, P):
+                for r in range(2):
+                    nc.tensor.matmul(
+                        bank_sum[:, c : c + P], lhsT=parts[r][:, c0 + c : c0 + c + P], rhs=ident[:],
+                        start=(r == 0), stop=(r == 1), is_transpose=True,
                     )
-                    parts.append(part)
-                res = keep.tile([P, t1 - t0], F32, name="res%d_%d" % (half, t0))
-                nc.vector.tensor_tensor(res[:], parts[0][:], parts[1][:], ADD)
-                nc.sync.dma_start(out[half * P : (half + 1) * P, t0:t1], res[:])
+            turned = keep.tile([P, width], F32, name="turned%d_%d" % (half, t0 + c0))
+            nc.scalar.copy(turned[:], bank_sum[:, 0:width])
+            for c in range(0, width, P):
+                nc.tensor.transpose(bank_back[:, c : c + P], turned[:, c : c + P], ident[:])
+            res = keep.tile([P, width], F32, name="res%d_%d" % (half, t0 + c0))
+            nc.scalar.copy(res[:], bank_back[:, 0:width])
+            nc.sync.dma_start(out[half * P : (half + 1) * P, t0 + c0 : t0 + c1], res[:])
+
+        add_on_tensor(0, 0, weighted(0, 0, 384), 0, 384, bank_b[0], bank_b[1])
+        add_on_tensor(0, 384, weighted(0, 384, T), 0, T - 384, bank_b[2], bank_b[3])
+        for t0, t1 in ((0, 384), (384, T)):
+            parts = weighted(1, t0, t1)
+            res = keep.tile([P, t1 - t0], F32, name="res1_%d" % t0)
+            nc.vector.tensor_tensor(res[:], parts[0][:], parts[1][:], ADD)
+            nc.sync.dma_start(out[P : 2 * P, t0:t1], res[:])

from contextlib import ExitStack

import concourse.mybir as mybir
from concourse.masks import make_identity

F32 = mybir.dt.float32
BF16 = mybir.dt.bfloat16
I32 = mybir.dt.int32
U32 = mybir.dt.uint32
U16 = mybir.dt.uint16
U8 = mybir.dt.uint8
FP8X4 = mybir.dt.float8_e4m3fn_x4
FP4X4 = mybir.dt.float4_e2m1fn_x4
MULT = mybir.AluOpType.mult
ADD = mybir.AluOpType.add
RELU = mybir.ActivationFunctionType.Relu

P = 128
T, E, C, H, N, HOT = 640, 10, 128, 512, 256, 5
S = E * C
FLOPS = 2 * S * (512 * H * 2 + H * N)

ORDER = [5, 6, 7, 8, 9, 0, 1, 2, 3, 4]
GATHERS = [(5, 7, 0, -1), (7, 10, 1, -1), (0, 3, 2, 0), (3, 5, 0, 1)]
B_BANK = [0, 2, 1, 3, 0, 4, 1, 2, 0, 3]
TURN_GROUPS = [(0, 2), (2, 4), (4, 6), (6, 8), (8, 9), (9, 10)]
QUANT_GROUPS = [(0, 4), (4, 8), (8, 9), (9, 10)]
TURN_LAG = 3
QUANT_LAG = 4


def tile_moe_hot_glu_relu_kernel(
    tc, x_words, x_scales, w1h_words, w1h_scales, w3h_words, w3h_scales, w2h_words, w2h_scales,
    w1c_words, w1c_scales, w3c_words, w3c_scales, w2c_words, w2c_scales, gate, offs, pos1, pos2, out,
):
    nc = tc.nc
    with ExitStack() as ctx:
        keep = ctx.enter_context(tc.tile_pool(name="keep", bufs=1))
        psum = ctx.enter_context(tc.psum_pool(name="psum", bufs=1))

        def plane(name, width, engine):
            t = keep.tile([P, HOT, width], U8, name=name, align_bytes=64)
            engine.memset(t[:].bitcast(I32), 0)
            return t

        def scale_loads(t, row0, src, width):
            rows = src.rearrange("e s b c -> b (e s) c").bitcast(I32)
            dst = t[:].bitcast(I32)
            return [(dst[row0 + r : P : 32, :, 0 : width // 4], rows[r:16:4, :, :]) for r in range(4)]

        words = {}

        def weight_load(key, src, e0, e1):
            if key[-1] == "h":
                view = src.rearrange("e s p c d -> p (e s) (c d)")
                first = 0
            else:
                view = src.rearrange("e s p c -> p (e s) c")
                first = HOT
            t = keep.tile([P, e1 - e0, view.shape[2]], U8, name="%s_%d" % (key, e0), align_bytes=64)
            for e in range(e0, e1):
                words[(key[:2], first + e)] = t[:, e - e0, :]
            return (t[:].bitcast(I32), view[:, e0:e1, :].bitcast(I32))

        offs_t = keep.tile([P, S // 16], U16, name="offs_t")
        pos1_t = keep.tile([P, T // 16], U16, name="pos1_t")
        pos2_t = keep.tile([P, T // 16], U16, name="pos2_t")
        x_w = keep.tile([P, T], U32, name="x_w", align_bytes=64)
        x_plane = keep.tile([P, T], U8, name="x_plane", align_bytes=64)

        xs_rows = x_scales.rearrange("s b t -> (s b) t").bitcast(I32)
        nc.sync.dma_start(offs_t[:], offs)
        for q in range(4):
            queue = nc.sync if q == 0 else nc.scalar
            queue.dma_start(
                x_plane[:].bitcast(I32)[32 * q : 32 * (q + 1), :],
                xs_rows[4 * q : 4 * (q + 1), :].unsqueeze(0).broadcast_to([8, 4, T // 4]),
            )
        nc.sync.dma_start(x_w[:].bitcast(I32), x_words.rearrange("s p t d -> p (s t d)").bitcast(I32))
        ident = keep.tile([P, P], F32, name="ident")
        make_identity(nc, ident[:])
        warm = keep.tile([P, 16], F32, name="warm")
        nc.vector.memset(warm[:, 0:8], 0.0)
        nc.scalar.activation(warm[:, 8:16], warm[:, 0:8], RELU)

        s_hot = plane("s_hot", H, nc.vector)
        s1c = plane("s1c", H, nc.vector)
        s3c = plane("s3c", H, nc.vector)
        s2 = plane("s2", N, nc.gpsimd)
        s2c_loads = scale_loads(s2, 0, w2c_scales, N)
        for dst, src in scale_loads(s_hot, 4, w1h_scales, H):
            nc.scalar.dma_start(dst, src)
        for dst, src in scale_loads(s_hot, 8, w3h_scales, H) + s2c_loads[:2]:
            nc.gpsimd.dma_start(dst, src)

        gate_t = keep.tile([P, 2, T], F32, name="gate_t")
        loads = [weight_load("w1c", w1c_words, 0, 2), weight_load("w3c", w3c_words, 0, 2)]
        loads += scale_loads(s1c, 0, w1c_scales, H) + scale_loads(s3c, 0, w3c_scales, H)
        loads += [weight_load("w1c", w1c_words, 2, 5), weight_load("w3c", w3c_words, 2, 5)]
        for e in range(HOT):
            loads += [weight_load("w1h", w1h_words, e, e + 1), weight_load("w3h", w3h_words, e, e + 1)]
        loads += [weight_load("w2c", w2c_words, 0, 5)] + s2c_loads[2:] + scale_loads(s2, 4, w2h_scales, N)
        loads += [weight_load("w2h", w2h_words, 0, 3), weight_load("w2h", w2h_words, 3, 5)]
        loads += [(pos1_t[:], pos1), (pos2_t[:], pos2), (gate_t[:], gate.rearrange("r p t -> p r t"))]
        for dst, src in loads:
            nc.sync.dma_start(dst, src)

        bank_a = [psum.tile([P, H], F32, name="bank_a%d" % j) for j in range(2)]
        bank_b = [psum.tile([P, H], F32, name="bank_b%d" % j) for j in range(5)]
        bank_y = psum.tile([P, H], F32, name="bank_y")

        x_codes = {}
        x_bytes = {}
        gathered = {}

        def gather(e0, e1, buffer):
            n = (e1 - e0) * C
            cols = offs_t[:, e0 * C // 16 : e1 * C // 16]
            if buffer not in gathered:
                gathered[buffer] = (
                    keep.tile([P, n], U8, name="gb%d" % buffer, align_bytes=64),
                    keep.tile([P, n], U32, name="gw%d" % buffer, align_bytes=64),
                )
            gb, gw = gathered[buffer]
            nc.vector.tensor_copy(gb[:], x_plane[:].indirect(cols))
            nc.vector.tensor_copy(gw[:], x_w[:].indirect(cols))
            for e in range(e0, e1):
                x_codes[e] = gw[:, (e - e0) * C : (e - e0 + 1) * C]
                x_bytes[e] = gb[:, (e - e0) * C : (e - e0 + 1) * C]

        def fmt(e):
            return FP8X4 if e < HOT else FP4X4

        h_tiles = {}
        grouped = {}
        h_codes = {}
        h_bytes = {}
        for s0, s1 in QUANT_GROUPS:
            grouped[s0] = keep.tile([P, (s1 - s0) * H], BF16, name="grouped%d" % s0, align_bytes=64)

        def first_layer(step):
            e = ORDER[step]
            a = bank_a[step % 2]
            b = bank_b[B_BANK[step]]
            sc1 = s_hot[4:P, e, :] if e < HOT else s1c[:, e - HOT, :]
            sc3 = s_hot[8:P, e, :] if e < HOT else s3c[:, e - HOT, :]
            for acc, key, sc in ((a, "w1", sc1), (b, "w3", sc3)):
                nc.tensor.matmul_mx(
                    acc[:], lhsT=x_codes[e].bitcast(FP8X4), lhsT_scale=x_bytes[e],
                    rhs=words[(key, e)].bitcast(fmt(e)), rhs_scale=sc, start=True, stop=True,
                )
            r = keep.tile([P, H], F32, name="r%d" % e)
            nc.scalar.activation(
                r[:].rearrange("s (u p d) -> s u p d", u=2, d=2),
                a[:].rearrange("s (p u d) -> s u p d", u=2, d=2), RELU,
            )
            h = keep.tile([P, H], BF16, name="h%d" % e, align_bytes=64)
            nc.vector.tensor_tensor(
                h[:].rearrange("s (u p d) -> s u p d", u=2, d=2),
                b[:].rearrange("s (p u d) -> s u p d", u=2, d=2),
                r[:].rearrange("s (u p d) -> s u p d", u=2, d=2), MULT,
            )
            h_tiles[step] = h

        def turn(s0, s1):
            q0 = [g for g in QUANT_GROUPS if g[0] <= s0 < g[1]][0][0]
            bank = bank_b[B_BANK[s1 - 1]]
            for step in range(s0, s1):
                pairs = h_tiles[step][:].bitcast(F32)
                for u in range(2):
                    col = (2 * (step - s0) + u) * C
                    nc.tensor.transpose(bank[:, col : col + C], pairs[:, u * P : (u + 1) * P], ident[:])
            nc.scalar.copy(
                grouped[q0][:, (s0 - q0) * H : (s1 - q0) * H].bitcast(F32).rearrange("p (e s u) -> p e s u", s=C, u=2),
                bank[:, 0 : (s1 - s0) * 2 * C].rearrange("p (e u s) -> p e s u", s=C, u=2),
            )

        def quantise(s0, s1):
            codes = keep.tile([P, (s1 - s0) * C], U32, name="codes%d" % s0, align_bytes=64)
            scales = keep.tile([P, (s1 - s0) * C], U8, name="scales%d" % s0, align_bytes=64)
            nc.vector.quantize_mx(codes[:].bitcast(FP8X4), scales[:], grouped[s0][:])
            for step in range(s0, s1):
                h_codes[ORDER[step]] = codes[:, (step - s0) * C : (step - s0 + 1) * C]
                h_bytes[ORDER[step]] = scales[:, (step - s0) * C : (step - s0 + 1) * C]

        y = [keep.tile([P, S], F32, name="y%d" % half) for half in range(2)]

        def second_layer(half, e0, e1, bank, copy):
            for e in range(e0, e1):
                w = words[("w2", e)]
                size = w.shape[1] // 2
                cols = slice(half * P, (half + 1) * P)
                sc = s2[4:P, e, cols] if e < HOT else s2[:, e - HOT, cols]
                nc.tensor.matmul_mx(
                    bank[:, (e - e0) * C : (e - e0 + 1) * C],
                    lhsT=w[:, half * size : (half + 1) * size].bitcast(fmt(e)), lhsT_scale=sc,
                    rhs=h_codes[e].bitcast(FP8X4), rhs_scale=h_bytes[e], start=True, stop=True,
                )
            copy(y[half][:, e0 * C : e1 * C], bank[:, 0 : (e1 - e0) * C])

        for step in range(-1, E + QUANT_LAG):
            if 0 <= step < E:
                first_layer(step)
            for e0, e1, buffer, behind in GATHERS:
                if behind == step:
                    gather(e0, e1, buffer)
            for s0, s1 in TURN_GROUPS:
                if s1 - 1 + TURN_LAG == step:
                    turn(s0, s1)
            for s0, s1 in QUANT_GROUPS:
                if s1 - 1 + QUANT_LAG == step:
                    quantise(s0, s1)
        second_layer(0, 5, 9, bank_y, nc.scalar.copy)
        second_layer(0, 9, 10, bank_b[1], nc.scalar.copy)
        second_layer(0, 0, 4, bank_a[0], nc.vector.tensor_copy)
        second_layer(0, 4, 5, bank_a[1], nc.scalar.copy)
        second_layer(1, 8, 10, bank_a[1], nc.scalar.copy)
        second_layer(1, 0, 4, bank_a[0], nc.scalar.copy)
        second_layer(1, 4, 8, bank_a[1], nc.scalar.copy)

        def weighted(half, t0, t1):
            parts = []
            for r, pos_t in enumerate((pos1_t, pos2_t)):
                part = keep.tile([P, t1 - t0], F32, name="part%d_%d_%d" % (half, t0, r))
                nc.vector.tensor_tensor(
                    part[:], y[half][:].indirect(pos_t[:, t0 // 16 : t1 // 16]), gate_t[:, r, t0:t1], MULT
                )
                parts.append(part)
            return parts

        def add_on_tensor(half, t0, parts, c0, c1, bank_sum, bank_back):
            width = c1 - c0
            for c in range(0, width, P):
                for r in range(2):
                    nc.tensor.matmul(
                        bank_sum[:, c : c + P], lhsT=parts[r][:, c0 + c : c0 + c + P], rhs=ident[:],
                        start=(r == 0), stop=(r == 1), is_transpose=True,
                    )
            turned = keep.tile([P, width], F32, name="turned%d_%d" % (half, t0 + c0))
            nc.scalar.copy(turned[:], bank_sum[:, 0:width])
            for c in range(0, width, P):
                nc.tensor.transpose(bank_back[:, c : c + P], turned[:, c : c + P], ident[:])
            res = keep.tile([P, width], F32, name="res%d_%d" % (half, t0 + c0))
            nc.scalar.copy(res[:], bank_back[:, 0:width])
            nc.sync.dma_start(out[half * P : (half + 1) * P, t0 + c0 : t0 + c1], res[:])

        add_on_tensor(0, 0, weighted(0, 0, 384), 0, 384, bank_b[0], bank_b[1])
        add_on_tensor(0, 384, weighted(0, 384, T), 0, T - 384, bank_b[2], bank_b[3])
        for t0, t1 in ((0, 384), (384, T)):
            parts = weighted(1, t0, t1)
            res = keep.tile([P, t1 - t0], F32, name="res1_%d" % t0)
            nc.vector.tensor_tensor(res[:], parts[0][:], parts[1][:], ADD)
            nc.sync.dma_start(out[P : 2 * P, t0:t1], res[:])
